import numpy as np
import ml_dtypes


def mxq(x, axis, fmt="e4m3"):
    dtype, down = {"e4m3": (ml_dtypes.float8_e4m3fn, 7), "e5m2": (ml_dtypes.float8_e5m2, 14)}[fmt]
    v = np.moveaxis(np.asarray(x, np.float32).astype(ml_dtypes.bfloat16).astype(np.float64), axis, -1)
    blocks = v.reshape(v.shape[:-1] + (-1, 32))
    amax = np.abs(blocks).max(-1, keepdims=True)
    byte = np.maximum(np.where(amax > 0, np.frexp(amax)[1] - 1 + 127, 0) - down, 1)
    scale = np.exp2(byte - 127.0)
    codes = (blocks / scale).astype(np.float32).astype(dtype).astype(np.float64)
    return np.moveaxis((codes * scale).reshape(v.shape), -1, axis)


WIDE = False


def mx_kscale(k):
    if not WIDE:
        return np.ones(k)
    levels = np.array([10, -10, 5, -5, 0])
    if k % 512:
        return np.exp2(np.random.permutation(np.resize(levels, k // 32))).repeat(32)
    a = np.empty((k // 512, 16))
    for p in range(k // 512):
        a[p, :8] = np.random.permutation(np.resize(levels, 8))
        for g in range(8):
            far = levels[np.abs(levels - a[p, g]) >= 10]
            a[p, g + 8] = far[np.random.randint(len(far))]
    return np.exp2(a.ravel()).repeat(32)


def f64(x):
    return np.asarray(x).astype(np.float64)


def striped(idx):
    return np.tile(idx.reshape(-1, 16).T, (8, 1)).astype(np.uint16)


def unstriped(offs):
    return offs[:16].T.reshape(-1).astype(np.int64)


E2M1 = np.array([0.0, 0.5, 1.0, 1.5, 2.0, 3.0, 4.0, 6.0, -0.0, -0.5, -1.0, -1.5, -2.0, -3.0, -4.0, -6.0])


def pack_weight(w, fmt):
    k, n = w.shape
    w = f64(np.asarray(w, np.float32).astype(ml_dtypes.bfloat16)).reshape(k // 32, 32, n)
    amax = np.abs(w).max(1)
    if fmt == "e4m3":
        byte = np.frexp(amax)[1] - 1 + 127 - 7
    else:
        mant, ex = np.frexp(amax / 6.0)
        byte = np.where(mant > 0.5, ex, ex - 1) + 127
    byte = np.clip(np.where(amax > 0, byte, 1), 1, 254)
    scaled = (w * np.exp2(127.0 - byte)[:, None, :]).reshape(k, n).astype(np.float32)
    by_word = np.ascontiguousarray(scaled.reshape(k // 512, 128, 4, n).transpose(0, 1, 3, 2))
    if fmt == "e4m3":
        words = by_word.astype(ml_dtypes.float8_e4m3fn).view(np.uint8)
    else:
        c = by_word.astype(ml_dtypes.float4_e2m1fn).view(np.uint8) & 0xF
        words = (c[..., 0::2] | (c[..., 1::2] << 4)).reshape(k // 512, 128, 2 * n)
    return np.ascontiguousarray(words), np.ascontiguousarray(byte.astype(np.uint8).reshape(k // 512, 16, n))


def unpack_weight(words, scales, fmt):
    g, _, n = scales.shape
    words = np.ascontiguousarray(words).reshape(g, 128, n, -1)
    if fmt == "e4m3":
        vals = words.view(ml_dtypes.float8_e4m3fn).astype(np.float64)
    else:
        nib = np.empty((g, 128, n, 4), np.uint8)
        nib[..., 0::2] = words & 0xF
        nib[..., 1::2] = words >> 4
        vals = E2M1[nib]
    vals = vals * np.repeat(np.exp2(scales.astype(np.float64) - 127.0), 8, axis=1)[..., None]
    return vals.transpose(0, 1, 3, 2).reshape(g * 512, n)


def gelu(v):
    return 0.5 * v * (1.0 + np.tanh(np.sqrt(2.0 / np.pi) * (v + 0.044715 * v**3)))


K, T, S, H, N = 1024, 2048, 1024, 1024, 512

def setup_inputs():
    n = np.random.standard_normal
    s = mx_kscale(K)[:, None]
    u = mx_kscale(H)[:, None]
    tab_words, tab_scales = pack_weight(n((K, T)) * s, "e4m3")
    w4_words, w4_scales = pack_weight(2.0 * n((H, N)) / np.sqrt(H) / u, "e2m1")
    gates = u / (1.0 + np.exp(-1.5 * n((H, T))))
    return {
        "tab_words": tab_words,
        "tab_scales": tab_scales,
        "offs": striped(np.random.permutation(T)[:S]),
        "w1": (1.5 * n((K, H)) / np.sqrt(K) / s).astype(np.float32),
        "b1": (0.5 * n(H)).astype(np.float32),
        "gT": gates.astype(np.float32),
        "w4_words": w4_words,
        "w4_scales": w4_scales,
        "b2": (0.3 * n(N)).astype(np.float32),
    }

def reference(tab_words, tab_scales, offs, w1, b1, gT, w4_words, w4_scales, b2):
    v = unpack_weight(tab_words, tab_scales, "e4m3")[:, unstriped(offs)]
    g = f64(gT)[:, unstriped(offs)]
    w1q = mxq(f64(w1), 0, "e4m3")
    a = (w1q.T @ v) + f64(b1)[:, None]
    h = g / (1.0 + np.exp(-a))
    hq = mxq(h, 0, "e4m3")
    w4 = unpack_weight(w4_words, w4_scales, "e2m1")
    return (w4.T @ hq) + f64(b2)[:, None]

@@ -1,0 +1,238 @@
+from contextlib import ExitStack
+
+import concourse.mybir as mybir
+
+K, T, S, H, N = 1024, 2048, 1024, 1024, 512
+FLOPS = 2 * K * H * S + 2 * H * N * S
+
+F32 = mybir.dt.float32
+BF16 = mybir.dt.bfloat16
+I32 = mybir.dt.int32
+U32 = mybir.dt.uint32
+U16 = mybir.dt.uint16
+U8 = mybir.dt.uint8
+FP8X4 = mybir.dt.float8_e4m3fn_x4
+FP4X4 = mybir.dt.float4_e2m1fn_x4
+ACT = mybir.ActivationFunctionType
+ALU = mybir.AluOpType
+
+P = 128
+PACK = 4
+KP = P * PACK
+PASSES = 2
+HALF = 512
+ROW = 8192
+
+
+def tile_list_click_gated_features_kernel(tc, tab_words, tab_scales, offs, w1, b1, gT, w4_words, w4_scales, b2, out):
+    nc = tc.nc
+    with ExitStack() as ctx:
+        keep = ctx.enter_context(tc.tile_pool(name="keep", bufs=1))
+        stage = ctx.enter_context(tc.tile_pool(name="stage", bufs=1))
+        late = ctx.enter_context(tc.tile_pool(name="late", bufs=1))
+        psum = ctx.enter_context(tc.psum_pool(name="psum", bufs=8))
+
+        offsets = keep.tile([P, S // 16], U16, name="offsets")
+        nc.sync.dma_start(offsets[:], offs)
+
+        def picks(lo, hi):
+            return offsets[:, lo // 16 : hi // 16]
+
+        tab_sc = keep.tile([P, T // 4], I32, name="tab_sc", align_bytes=64)
+        nc.vector.memset(tab_sc[:], 0)
+        for q in range(4):
+            nc.scalar.dma_start(out=tab_sc[32 * q : 32 * q + 8, :], in_=tab_scales[:, 4 * q : 4 * q + 4, :].bitcast(I32))
+        warm = late.tile([P, 13 * T + 1024], F32, name="warm", offset=0, align_bytes=64)
+        nc.vector.memset(warm[:, 0:1], 0.0)
+        nc.scalar.activation(out=warm[:, 1:2], in_=warm[:, 0:1], func=ACT.Sigmoid)
+        w4_sc = late.tile([P, PASSES, N // 4], I32, name="w4_sc", align_bytes=64, offset=13 * ROW)
+        nc.vector.memset(w4_sc[:], 0)
+
+        tab_w = [keep.tile([P, T], I32, name="tab_w0", align_bytes=64), late.tile([P, T], I32, name="tab_w1", align_bytes=64, offset=4 * ROW)]
+        w_raw = {}
+        gates = [late.tile([P, T], F32, name=f"gates{i}", align_bytes=64, offset=(5 + i) * ROW) for i in range(8)]
+
+        def load_w1(b, a):
+            if (b, a) == (0, 0):
+                raw = keep.tile([P, PACK, KP], F32, name="w_raw_first", align_bytes=64)
+            else:
+                raw = late.tile([P, PACK, KP], F32, name=f"w_raw{b}{a}", align_bytes=64, offset=(2 * b + a - 1) * ROW)
+            nc.sync.dma_start(out=raw[:], in_=w1[a * KP : (a + 1) * KP, b * KP : (b + 1) * KP].rearrange("(p j) c -> p j c", j=PACK))
+            w_raw[b, a] = raw
+
+        def load_words(a):
+            nc.sync.dma_start(out=tab_w[a][:], in_=tab_words[a].rearrange("p t i -> p (t i)").bitcast(I32))
+
+        def load_gates(i):
+            b, t = divmod(i, PACK)
+            nc.sync.dma_start(out=gates[i][:], in_=gT[b * KP : (b + 1) * KP, :].rearrange("(p t) c -> p t c", t=PACK)[:, t, :])
+
+        b1_sb = late.tile([P, PASSES, PACK], F32, name="b1_sb", align_bytes=64, offset=13 * ROW + 1024)
+        b2_sb = late.tile([P, N // P], F32, name="b2_sb", align_bytes=64, offset=13 * ROW + 1088)
+        w4_w = late.tile([P, PASSES, 2 * N // 4], I32, name="w4_w", align_bytes=64, offset=13 * ROW + 2048)
+
+        load_words(0)
+        load_w1(0, 0)
+        load_w1(0, 1)
+        nc.sync.dma_start(out=b1_sb[:], in_=b1.rearrange("(b p t) -> p b t", b=PASSES, t=PACK))
+        load_words(1)
+        load_gates(0)
+        load_w1(1, 0)
+        load_gates(1)
+        load_w1(1, 1)
+        load_gates(2)
+        load_gates(3)
+        for q in range(4):
+            nc.sync.dma_start(out=w4_sc[32 * q : 32 * q + 4, :, :], in_=w4_scales[:, 4 * q : 4 * q + 4, :].bitcast(I32).rearrange("a r c -> r a c"))
+        nc.sync.dma_start(out=w4_w[:], in_=w4_words.bitcast(I32).rearrange("a p c -> p a c"))
+        with nc.allow_non_contiguous_dma(reason="one bias value to a partition"):
+            nc.sync.dma_start(out=b2_sb[:], in_=b2.rearrange("(c p) -> p c", p=P))
+        for i in range(4, 8):
+            load_gates(i)
+
+        v_sc = keep.tile([P, S], U8, name="v_sc", align_bytes=64)
+        v_w = [keep.tile([P, S], U32, name=f"v_w{a}", align_bytes=64) for a in range(PASSES)]
+        w_codes = keep.tile([P, PASSES, PASSES, KP], U32, name="w_codes", align_bytes=64)
+        w_sc = keep.tile([P, PASSES, PASSES, KP], U8, name="w_sc", align_bytes=64)
+        w_bf = {}
+
+        def round_w1(b, a, t0, t1, on_vector):
+            if (b, a) not in w_bf:
+                w_bf[b, a] = stage.tile([P, PACK, P, PACK], BF16, name="w_bf", tag="w_bf", bufs=2, align_bytes=64)
+            dst = w_bf[b, a][:, t0:t1, :, :].rearrange("p t m j -> p m j t")
+            src = w_raw[b, a][:].rearrange("p j (m t) -> p m j t", t=PACK)[:, :, :, t0:t1]
+            if on_vector:
+                nc.vector.tensor_copy(out=dst, in_=src)
+            else:
+                nc.scalar.copy(out=dst, in_=src)
+
+        def quantize_w1(b, a):
+            nc.vector.quantize_mx(out=w_codes[:, b, a, :].bitcast(FP8X4), scales=w_sc[:, b, a, :], in_=w_bf[b, a][:].rearrange("p t m j -> p (t m j)"))
+
+        def gather_words(a, lo, hi):
+            nc.vector.tensor_copy(v_w[a][:, lo:hi], tab_w[a][:].bitcast(U32).indirect(picks(lo, hi)))
+
+        sig = {}
+
+        def hidden(i, half):
+            b, t = divmod(i, PACK)
+            cols = slice(half * HALF, (half + 1) * HALF)
+            acc = psum.tile([P, HALF], F32, name="acc", tag="bank")
+            for a in range(PASSES):
+                nc.tensor.matmul_mx(
+                    out=acc[:],
+                    lhsT=w_codes[:, b, a, t * P : (t + 1) * P].bitcast(FP8X4),
+                    lhsT_scale=w_sc[:, b, a, t * P : (t + 1) * P],
+                    rhs=v_w[a][:, cols].bitcast(FP8X4),
+                    rhs_scale=v_sc[4 * a : P, cols],
+                    start=(a == 0),
+                    stop=(a == PASSES - 1),
+                )
+            if i not in sig:
+                sig[i] = stage.tile([P, S], F32, name="sig", tag="sig", bufs=6, align_bytes=64)
+            nc.scalar.activation(out=sig[i][:, cols], in_=acc[:], func=ACT.Sigmoid, bias=b1_sb[:, b, t : t + 1])
+
+        h32 = [keep.tile([P, PACK, S], F32, name=f"h32_{b}", align_bytes=64) for b in range(PASSES)]
+        h_bf = [keep.tile([P, S, PACK], BF16, name=f"h_bf{b}", align_bytes=64) for b in range(PASSES)]
+        h_codes = keep.tile([P, PASSES, S], U32, name="h_codes", align_bytes=64)
+        h_sc = keep.tile([P, PASSES, S], U8, name="h_sc", align_bytes=64)
+
+        def gate(i, lo, hi):
+            b, t = divmod(i, PACK)
+            nc.vector.tensor_tensor(h32[b][:, t, lo:hi], gates[i][:].indirect(picks(lo, hi)), sig[i][:, lo:hi], ALU.mult)
+
+        def round_h(b, lo, hi, on_vector):
+            dst = h_bf[b][:, lo:hi, :].rearrange("p (c i) t -> p c t i", i=4)
+            src = h32[b][:, :, lo:hi].rearrange("p t (c i) -> p c t i", i=4)
+            if on_vector:
+                nc.vector.tensor_copy(out=dst, in_=src)
+            else:
+                nc.scalar.copy(out=dst, in_=src)
+
+        def quantize_h(b, half):
+            cols = slice(half * HALF, (half + 1) * HALF)
+            nc.vector.quantize_mx(out=h_codes[:, b, cols].bitcast(FP8X4), scales=h_sc[:, b, cols], in_=h_bf[b][:, cols, :].rearrange("p s t -> p (s t)"))
+
+        sums = {}
+
+        def project(b, half):
+            cols = slice(half * HALF, (half + 1) * HALF)
+            for c in range(N // P):
+                if b == 0:
+                    sums[c, half] = psum.tile([P, HALF], F32, name="total", tag="bank")
+                nc.tensor.matmul_mx(
+                    out=sums[c, half][:],
+                    lhsT=w4_w[:, b, :].bitcast(U8)[:, 2 * c * P : 2 * (c + 1) * P].bitcast(FP4X4),
+                    lhsT_scale=w4_sc[:, b, :].bitcast(U8)[:, c * P : (c + 1) * P],
+                    rhs=h_codes[:, b, cols].bitcast(FP8X4),
+                    rhs_scale=h_sc[:, b, cols],
+                    start=(b == 0),
+                    stop=(b == PASSES - 1),
+                )
+
+        results = {}
+
+        def finish(c, half, on_vector):
+            if half not in results:
+                results[half] = late.tile([P, PACK, KP], F32, name=f"result{half}", align_bytes=64, offset=(3 * (1 - half)) * ROW)
+            dst = results[half][:, c, :]
+            if on_vector:
+                nc.vector.tensor_scalar(out=dst, in0=sums[c, half][:], scalar1=b2_sb[:, c : c + 1], scalar2=None, op0=ALU.add)
+            else:
+                nc.scalar.activation(out=dst, in_=sums[c, half][:], func=ACT.Identity, bias=b2_sb[:, c : c + 1])
+            nc.sync.dma_start(out=out[c * P : (c + 1) * P, half * HALF : (half + 1) * HALF], in_=dst)
+
+        gather_words(0, 0, S)
+        nc.vector.tensor_copy(v_sc[:], tab_sc[:].bitcast(U8).indirect(offsets[:]))
+        round_w1(0, 0, 0, 4, False)
+        quantize_w1(0, 0)
+        round_w1(0, 1, 0, 2, False)
+        round_w1(0, 1, 2, 4, True)
+        quantize_w1(0, 1)
+        gather_words(1, 0, HALF)
+        gather_words(1, HALF, S)
+        for i in range(4):
+            hidden(i, 0)
+            hidden(i, 1)
+        gate(0, 0, HALF)
+        gate(0, HALF, S)
+        round_w1(1, 0, 0, 2, False)
+        round_w1(1, 0, 2, 4, True)
+        quantize_w1(1, 0)
+        gate(1, 0, S)
+        round_w1(1, 1, 0, 2, False)
+        round_w1(1, 1, 2, 4, True)
+        quantize_w1(1, 1)
+        gate(2, 0, S)
+        hidden(4, 0)
+        hidden(4, 1)
+        gate(3, 0, HALF)
+        gate(3, HALF, S)
+        round_h(0, 0, HALF, False)
+        gate(4, 0, S)
+        hidden(5, 0)
+        hidden(5, 1)
+        round_h(0, HALF, S, False)
+        gate(5, 0, S)
+        for i in range(6, 8):
+            hidden(i, 0)
+            hidden(i, 1)
+        quantize_h(0, 0)
+        quantize_h(0, 1)
+        project(0, 0)
+        project(0, 1)
+        gate(6, 0, S)
+        gate(7, 0, 256)
+        round_h(1, 0, 256, False)
+        gate(7, 256, HALF)
+        round_h(1, 256, HALF, True)
+        quantize_h(1, 0)
+        project(1, 0)
+        gate(7, HALF, S)
+        round_h(1, HALF, S, True)
+        quantize_h(1, 1)
+        project(1, 1)
+        for c in range(N // P):
+            finish(c, 0, False)
+        for c in range(N // P):
+            finish(c, 1, c % 2 == 0)

@@ -22,6 +22,7 @@ KP = P * PACK
 PASSES = 2
 HALF = 512
 ROW = 8192
+SIG_AT = 13 * ROW + 4096
 
 
 def tile_list_click_gated_features_kernel(tc, tab_words, tab_scales, offs, w1, b1, gT, w4_words, w4_scales, b2, out):
@@ -76,10 +77,10 @@ def tile_list_click_gated_features_kernel(tc, tab_words, tab_scales, offs, w1, b
         load_w1(0, 1)
         nc.sync.dma_start(out=b1_sb[:], in_=b1.rearrange("(b p t) -> p b t", b=PASSES, t=PACK))
         load_words(1)
-        load_gates(0)
         load_w1(1, 0)
-        load_gates(1)
         load_w1(1, 1)
+        load_gates(0)
+        load_gates(1)
         load_gates(2)
         load_gates(3)
         for q in range(4):
@@ -128,18 +129,23 @@ def tile_list_click_gated_features_kernel(tc, tab_words, tab_scales, offs, w1, b
                     start=(a == 0),
                     stop=(a == PASSES - 1),
                 )
-            if i not in sig:
-                sig[i] = stage.tile([P, S], F32, name="sig", tag="sig", bufs=6, align_bytes=64)
-            nc.scalar.activation(out=sig[i][:, cols], in_=acc[:], func=ACT.Sigmoid, bias=b1_sb[:, b, t : t + 1])
+            at = SIG_AT + (i % 6) * 4096
+            if i >= 6:
+                sig[i, half] = late.tile([P, HALF], F32, name=f"sig{i}_{half}", align_bytes=64, offset=at + half * 2048)[:]
+            else:
+                if half == 0:
+                    sig[i] = late.tile([P, S], F32, name=f"sig{i}", align_bytes=64, offset=at)
+                sig[i, half] = sig[i][:, cols]
+            nc.scalar.activation(out=sig[i, half], in_=acc[:], func=ACT.Sigmoid, bias=b1_sb[:, b, t : t + 1])
 
         h32 = [keep.tile([P, PACK, S], F32, name=f"h32_{b}", align_bytes=64) for b in range(PASSES)]
         h_bf = [keep.tile([P, S, PACK], BF16, name=f"h_bf{b}", align_bytes=64) for b in range(PASSES)]
-        h_codes = keep.tile([P, PASSES, S], U32, name="h_codes", align_bytes=64)
+        h_codes = {}
         h_sc = keep.tile([P, PASSES, S], U8, name="h_sc", align_bytes=64)
 
         def gate(i, lo, hi):
             b, t = divmod(i, PACK)
-            nc.vector.tensor_tensor(h32[b][:, t, lo:hi], gates[i][:].indirect(picks(lo, hi)), sig[i][:, lo:hi], ALU.mult)
+            nc.vector.tensor_tensor(h32[b][:, t, lo:hi], gates[i][:].indirect(picks(lo, hi)), sig[i, lo // HALF][:, lo % HALF : lo % HALF + hi - lo] if i >= 6 else sig[i][:, lo:hi], ALU.mult)
 
         def round_h(b, lo, hi, on_vector):
             dst = h_bf[b][:, lo:hi, :].rearrange("p (c i) t -> p c t i", i=4)
@@ -151,7 +157,11 @@ def tile_list_click_gated_features_kernel(tc, tab_words, tab_scales, offs, w1, b
 
         def quantize_h(b, half):
             cols = slice(half * HALF, (half + 1) * HALF)
-            nc.vector.quantize_mx(out=h_codes[:, b, cols].bitcast(FP8X4), scales=h_sc[:, b, cols], in_=h_bf[b][:, cols, :].rearrange("p s t -> p (s t)"))
+            if b == 0:
+                h_codes[b, half] = late.tile([P, HALF], U32, name=f"h_codes{b}{half}", align_bytes=64, offset=SIG_AT + half * 4096)
+            else:
+                h_codes[b, half] = keep.tile([P, HALF], U32, name=f"h_codes{b}{half}", align_bytes=64)
+            nc.vector.quantize_mx(out=h_codes[b, half][:].bitcast(FP8X4), scales=h_sc[:, b, cols], in_=h_bf[b][:, cols, :].rearrange("p s t -> p (s t)"))
 
         sums = {}
 
@@ -164,7 +174,7 @@ def tile_list_click_gated_features_kernel(tc, tab_words, tab_scales, offs, w1, b
                     out=sums[c, half][:],
                     lhsT=w4_w[:, b, :].bitcast(U8)[:, 2 * c * P : 2 * (c + 1) * P].bitcast(FP4X4),
                     lhsT_scale=w4_sc[:, b, :].bitcast(U8)[:, c * P : (c + 1) * P],
-                    rhs=h_codes[:, b, cols].bitcast(FP8X4),
+                    rhs=h_codes[b, half][:].bitcast(FP8X4),
                     rhs_scale=h_sc[:, b, cols],
                     start=(b == 0),
                     stop=(b == PASSES - 1),
@@ -191,18 +201,15 @@ def tile_list_click_gated_features_kernel(tc, tab_words, tab_scales, offs, w1, b
         quantize_w1(0, 1)
         gather_words(1, 0, HALF)
         gather_words(1, HALF, S)
+        round_w1(1, 0, 0, 4, True)
+        quantize_w1(1, 0)
+        round_w1(1, 1, 0, 4, True)
+        quantize_w1(1, 1)
         for i in range(4):
             hidden(i, 0)
             hidden(i, 1)
-        gate(0, 0, HALF)
-        gate(0, HALF, S)
-        round_w1(1, 0, 0, 2, False)
-        round_w1(1, 0, 2, 4, True)
-        quantize_w1(1, 0)
+        gate(0, 0, S)
         gate(1, 0, S)
-        round_w1(1, 1, 0, 2, False)
-        round_w1(1, 1, 2, 4, True)
-        quantize_w1(1, 1)
         gate(2, 0, S)
         hidden(4, 0)
         hidden(4, 1)
@@ -217,22 +224,25 @@ def tile_list_click_gated_features_kernel(tc, tab_words, tab_scales, offs, w1, b
         for i in range(6, 8):
             hidden(i, 0)
             hidden(i, 1)
+        gate(6, 0, HALF)
+        gate(6, HALF, S)
         quantize_h(0, 0)
-        quantize_h(0, 1)
         project(0, 0)
-        project(0, 1)
-        gate(6, 0, S)
         gate(7, 0, 256)
         round_h(1, 0, 256, False)
         gate(7, 256, HALF)
-        round_h(1, 256, HALF, True)
+        round_h(1, 256, HALF, False)
         quantize_h(1, 0)
         project(1, 0)
-        gate(7, HALF, S)
-        round_h(1, HALF, S, True)
+        gate(7, HALF, 768)
+        gate(7, 768, S)
+        quantize_h(0, 1)
+        project(0, 1)
+        round_h(1, HALF, 768, True)
+        round_h(1, 768, S, True)
         quantize_h(1, 1)
         project(1, 1)
         for c in range(N // P):
             finish(c, 0, False)
         for c in range(N // P):
-            finish(c, 1, c % 2 == 0)
+            finish(c, 1, c != 2)

@@ -68,14 +68,14 @@ def tile_list_click_gated_features_kernel(tc, tab_words, tab_scales, offs, w1, b
             b, t = divmod(i, PACK)
             nc.sync.dma_start(out=gates[i][:], in_=gT[b * KP : (b + 1) * KP, :].rearrange("(p t) c -> p t c", t=PACK)[:, t, :])
 
-        b1_sb = late.tile([P, PASSES, PACK], F32, name="b1_sb", align_bytes=64, offset=13 * ROW + 1024)
+        b1_sb = late.tile([P, PASSES, 2 * PACK], F32, name="b1_sb", align_bytes=64, offset=13 * ROW + 1024)
         b2_sb = late.tile([P, N // P], F32, name="b2_sb", align_bytes=64, offset=13 * ROW + 1088)
         w4_w = late.tile([P, PASSES, 2 * N // 4], I32, name="w4_w", align_bytes=64, offset=13 * ROW + 2048)
 
         load_words(0)
         load_w1(0, 0)
         load_w1(0, 1)
-        nc.sync.dma_start(out=b1_sb[:], in_=b1.rearrange("(b p t) -> p b t", b=PASSES, t=PACK))
+        nc.sync.dma_start(out=b1_sb[:, :, 0:PACK], in_=b1.rearrange("(b p t) -> p b t", b=PASSES, t=PACK))
         load_words(1)
         load_w1(1, 0)
         load_w1(1, 1)
@@ -85,11 +85,12 @@ def tile_list_click_gated_features_kernel(tc, tab_words, tab_scales, offs, w1, b
         load_gates(3)
         for q in range(4):
             nc.sync.dma_start(out=w4_sc[32 * q : 32 * q + 4, :, :], in_=w4_scales[:, 4 * q : 4 * q + 4, :].bitcast(I32).rearrange("a r c -> r a c"))
-        nc.sync.dma_start(out=w4_w[:], in_=w4_words.bitcast(I32).rearrange("a p c -> p a c"))
-        with nc.allow_non_contiguous_dma(reason="one bias value to a partition"):
-            nc.sync.dma_start(out=b2_sb[:], in_=b2.rearrange("(c p) -> p c", p=P))
+        nc.sync.dma_start(out=w4_w[:, 0, :], in_=w4_words[0].bitcast(I32))
         for i in range(4, 8):
             load_gates(i)
+        nc.sync.dma_start(out=w4_w[:, 1, :], in_=w4_words[1].bitcast(I32))
+        with nc.allow_non_contiguous_dma(reason="one bias value to a partition"):
+            nc.sync.dma_start(out=b2_sb[:], in_=b2.rearrange("(c p) -> p c", p=P))
 
         v_sc = keep.tile([P, S], U8, name="v_sc", align_bytes=64)
         v_w = [keep.tile([P, S], U32, name=f"v_w{a}", align_bytes=64) for a in range(PASSES)]
@@ -103,7 +104,7 @@ def tile_list_click_gated_features_kernel(tc, tab_words, tab_scales, offs, w1, b
             dst = w_bf[b, a][:, t0:t1, :, :].rearrange("p t m j -> p m j t")
             src = w_raw[b, a][:].rearrange("p j (m t) -> p m j t", t=PACK)[:, :, :, t0:t1]
             if on_vector:
-                nc.vector.tensor_copy(out=dst, in_=src)
+                nc.vector.tensor_copy(out=dst.rearrange("p m j t -> p m t j"), in_=src.rearrange("p m j t -> p m t j"))
             else:
                 nc.scalar.copy(out=dst, in_=src)
 
@@ -147,21 +148,23 @@ def tile_list_click_gated_features_kernel(tc, tab_words, tab_scales, offs, w1, b
             b, t = divmod(i, PACK)
             nc.vector.tensor_tensor(h32[b][:, t, lo:hi], gates[i][:].indirect(picks(lo, hi)), sig[i, lo // HALF][:, lo % HALF : lo % HALF + hi - lo] if i >= 6 else sig[i][:, lo:hi], ALU.mult)
 
-        def round_h(b, lo, hi, on_vector):
-            dst = h_bf[b][:, lo:hi, :].rearrange("p (c i) t -> p c t i", i=4)
-            src = h32[b][:, :, lo:hi].rearrange("p t (c i) -> p c t i", i=4)
+        def round_h(b, lo, hi, on_vector, t0=0, t1=PACK):
+            dst = h_bf[b][:, lo:hi, t0:t1].rearrange("p (c i) t -> p c t i", i=4)
+            src = h32[b][:, t0:t1, lo:hi].rearrange("p t (c i) -> p c t i", i=4)
             if on_vector:
                 nc.vector.tensor_copy(out=dst, in_=src)
             else:
                 nc.scalar.copy(out=dst, in_=src)
 
-        def quantize_h(b, half):
-            cols = slice(half * HALF, (half + 1) * HALF)
-            if b == 0:
-                h_codes[b, half] = late.tile([P, HALF], U32, name=f"h_codes{b}{half}", align_bytes=64, offset=SIG_AT + half * 4096)
-            else:
-                h_codes[b, half] = keep.tile([P, HALF], U32, name=f"h_codes{b}{half}", align_bytes=64)
-            nc.vector.quantize_mx(out=h_codes[b, half][:].bitcast(FP8X4), scales=h_sc[:, b, cols], in_=h_bf[b][:, cols, :].rearrange("p s t -> p (s t)"))
+        def quantize_h(b, lo, hi):
+            half = lo // HALF
+            if (b, half) not in h_codes:
+                if b == 0:
+                    h_codes[b, half] = late.tile([P, HALF], U32, name=f"h_codes{b}{half}", align_bytes=64, offset=SIG_AT + half * 4096)
+                else:
+                    h_codes[b, half] = keep.tile([P, HALF], U32, name=f"h_codes{b}{half}", align_bytes=64)
+            codes = h_codes[b, half][:, lo - half * HALF : hi - half * HALF]
+            nc.vector.quantize_mx(out=codes.bitcast(FP8X4), scales=h_sc[:, b, lo:hi], in_=h_bf[b][:, lo:hi, :].rearrange("p s t -> p (s t)"))
 
         sums = {}
 
@@ -224,23 +227,25 @@ def tile_list_click_gated_features_kernel(tc, tab_words, tab_scales, offs, w1, b
         for i in range(6, 8):
             hidden(i, 0)
             hidden(i, 1)
+        round_h(1, 0, S, False, 0, 2)
         gate(6, 0, HALF)
         gate(6, HALF, S)
-        quantize_h(0, 0)
+        quantize_h(0, 0, HALF)
         project(0, 0)
-        gate(7, 0, 256)
-        round_h(1, 0, 256, False)
-        gate(7, 256, HALF)
-        round_h(1, 256, HALF, False)
-        quantize_h(1, 0)
+        for lo in range(0, HALF, 128):
+            gate(7, lo, lo + 128)
+            round_h(1, lo, lo + 128, False, 2, 4)
+            if lo % 256 == 128:
+                quantize_h(1, lo - 128, lo + 128)
         project(1, 0)
-        gate(7, HALF, 768)
+        gate(7, 512, 640)
+        gate(7, 640, 768)
+        round_h(1, HALF, 768, False, 2, 4)
         gate(7, 768, S)
-        quantize_h(0, 1)
+        round_h(1, 768, S, True, 2, 4)
+        quantize_h(0, HALF, S)
         project(0, 1)
-        round_h(1, HALF, 768, True)
-        round_h(1, 768, S, True)
-        quantize_h(1, 1)
+        quantize_h(1, HALF, S)
         project(1, 1)
         for c in range(N // P):
             finish(c, 0, False)

@@ -69,7 +69,7 @@ def tile_list_click_gated_features_kernel(tc, tab_words, tab_scales, offs, w1, b
             nc.sync.dma_start(out=gates[i][:], in_=gT[b * KP : (b + 1) * KP, :].rearrange("(p t) c -> p t c", t=PACK)[:, t, :])
 
         b1_sb = late.tile([P, PASSES, 2 * PACK], F32, name="b1_sb", align_bytes=64, offset=13 * ROW + 1024)
-        b2_sb = late.tile([P, N // P], F32, name="b2_sb", align_bytes=64, offset=13 * ROW + 1088)
+        b2_sb = late.tile([P, N // P, 8], F32, name="b2_sb", align_bytes=64, offset=13 * ROW + 1088)
         w4_w = late.tile([P, PASSES, 2 * N // 4], I32, name="w4_w", align_bytes=64, offset=13 * ROW + 2048)
 
         load_words(0)
@@ -90,7 +90,7 @@ def tile_list_click_gated_features_kernel(tc, tab_words, tab_scales, offs, w1, b
             load_gates(i)
         nc.sync.dma_start(out=w4_w[:, 1, :], in_=w4_words[1].bitcast(I32))
         with nc.allow_non_contiguous_dma(reason="one bias value to a partition"):
-            nc.sync.dma_start(out=b2_sb[:], in_=b2.rearrange("(c p) -> p c", p=P))
+            nc.sync.dma_start(out=b2_sb[:, :, 0], in_=b2.rearrange("(c p) -> p c", p=P))
 
         v_sc = keep.tile([P, S], U8, name="v_sc", align_bytes=64)
         v_w = [keep.tile([P, S], U32, name=f"v_w{a}", align_bytes=64) for a in range(PASSES)]
@@ -104,7 +104,7 @@ def tile_list_click_gated_features_kernel(tc, tab_words, tab_scales, offs, w1, b
             dst = w_bf[b, a][:, t0:t1, :, :].rearrange("p t m j -> p m j t")
             src = w_raw[b, a][:].rearrange("p j (m t) -> p m j t", t=PACK)[:, :, :, t0:t1]
             if on_vector:
-                nc.vector.tensor_copy(out=dst.rearrange("p m j t -> p m t j"), in_=src.rearrange("p m j t -> p m t j"))
+                nc.vector.tensor_copy(out=dst, in_=src)
             else:
                 nc.scalar.copy(out=dst, in_=src)
 
@@ -190,9 +190,9 @@ def tile_list_click_gated_features_kernel(tc, tab_words, tab_scales, offs, w1, b
                 results[half] = late.tile([P, PACK, KP], F32, name=f"result{half}", align_bytes=64, offset=(3 * (1 - half)) * ROW)
             dst = results[half][:, c, :]
             if on_vector:
-                nc.vector.tensor_scalar(out=dst, in0=sums[c, half][:], scalar1=b2_sb[:, c : c + 1], scalar2=None, op0=ALU.add)
+                nc.vector.tensor_scalar(out=dst, in0=sums[c, half][:], scalar1=b2_sb[:, c, 0:1], scalar2=None, op0=ALU.add)
             else:
-                nc.scalar.activation(out=dst, in_=sums[c, half][:], func=ACT.Identity, bias=b2_sb[:, c : c + 1])
+                nc.scalar.activation(out=dst, in_=sums[c, half][:], func=ACT.Identity, bias=b2_sb[:, c, 0:1])
             nc.sync.dma_start(out=out[c * P : (c + 1) * P, half * HALF : (half + 1) * HALF], in_=dst)
 
         gather_words(0, 0, S)
@@ -204,9 +204,11 @@ def tile_list_click_gated_features_kernel(tc, tab_words, tab_scales, offs, w1, b
         quantize_w1(0, 1)
         gather_words(1, 0, HALF)
         gather_words(1, HALF, S)
-        round_w1(1, 0, 0, 4, True)
+        round_w1(1, 0, 0, 2, True)
+        round_w1(1, 0, 2, 4, True)
         quantize_w1(1, 0)
-        round_w1(1, 1, 0, 4, True)
+        round_w1(1, 1, 0, 2, True)
+        round_w1(1, 1, 2, 4, True)
         quantize_w1(1, 1)
         for i in range(4):
             hidden(i, 0)
@@ -227,7 +229,7 @@ def tile_list_click_gated_features_kernel(tc, tab_words, tab_scales, offs, w1, b
         for i in range(6, 8):
             hidden(i, 0)
             hidden(i, 1)
-        round_h(1, 0, S, False, 0, 2)
+        round_h(1, 0, HALF, False, 0, 2)
         gate(6, 0, HALF)
         gate(6, HALF, S)
         quantize_h(0, 0, HALF)
@@ -240,9 +242,9 @@ def tile_list_click_gated_features_kernel(tc, tab_words, tab_scales, offs, w1, b
         project(1, 0)
         gate(7, 512, 640)
         gate(7, 640, 768)
-        round_h(1, HALF, 768, False, 2, 4)
+        round_h(1, HALF, 768, False)
         gate(7, 768, S)
-        round_h(1, 768, S, True, 2, 4)
+        round_h(1, 768, S, True)
         quantize_h(0, HALF, S)
         project(0, 1)
         quantize_h(1, HALF, S)

@@ -18,20 +18,38 @@ ALU = mybir.AluOpType
 
 P = 128
 PACK = 4
-KP = P * PACK
+SPAN = P * PACK
 PASSES = 2
-HALF = 512
-ROW = 8192
-SIG_AT = 13 * ROW + 4096
+PLANES = PASSES * PACK
+QUADRANTS = 4
+HALF = S // 2
+QUARTER = S // 4
+CHUNK = S // 8
+BANK = 2048
+PAD = 8
+
+SLOT = 8192
+RAW_AT = 0
+RESULT_AT = (3 * SLOT, RAW_AT)
+WORDS_AT = 4 * SLOT
+GATES_AT = 5 * SLOT
+W4_SCALES_AT = GATES_AT + PLANES * SLOT
+B1_AT = W4_SCALES_AT + 1024
+B2_AT = B1_AT + 64
+W4_WORDS_AT = W4_SCALES_AT + 2048
+HELD_BYTES = W4_WORDS_AT + 2048
+SIG_AT = HELD_BYTES
+SIG_BYTES = 4 * S
+SIG_SLOTS = 6
 
 
 def tile_list_click_gated_features_kernel(tc, tab_words, tab_scales, offs, w1, b1, gT, w4_words, w4_scales, b2, out):
     nc = tc.nc
     with ExitStack() as ctx:
         keep = ctx.enter_context(tc.tile_pool(name="keep", bufs=1))
-        stage = ctx.enter_context(tc.tile_pool(name="stage", bufs=1))
-        late = ctx.enter_context(tc.tile_pool(name="late", bufs=1))
-        psum = ctx.enter_context(tc.psum_pool(name="psum", bufs=8))
+        ring = ctx.enter_context(tc.tile_pool(name="ring", bufs=1))
+        placed = ctx.enter_context(tc.tile_pool(name="placed", bufs=1))
+        psum = ctx.enter_context(tc.psum_pool(name="psum", bufs=1))
 
         offsets = keep.tile([P, S // 16], U16, name="offsets")
         nc.sync.dma_start(offsets[:], offs)
@@ -41,24 +59,30 @@ def tile_list_click_gated_features_kernel(tc, tab_words, tab_scales, offs, w1, b
 
         tab_sc = keep.tile([P, T // 4], I32, name="tab_sc", align_bytes=64)
         nc.vector.memset(tab_sc[:], 0)
-        for q in range(4):
+        for q in range(QUADRANTS):
             nc.scalar.dma_start(out=tab_sc[32 * q : 32 * q + 8, :], in_=tab_scales[:, 4 * q : 4 * q + 4, :].bitcast(I32))
-        warm = late.tile([P, 13 * T + 1024], F32, name="warm", offset=0, align_bytes=64)
+
+        warm = placed.tile([P, HELD_BYTES // 4], F32, name="warm", offset=0, align_bytes=64)
         nc.vector.memset(warm[:, 0:1], 0.0)
         nc.scalar.activation(out=warm[:, 1:2], in_=warm[:, 0:1], func=ACT.Sigmoid)
-        w4_sc = late.tile([P, PASSES, N // 4], I32, name="w4_sc", align_bytes=64, offset=13 * ROW)
+        w4_sc = placed.tile([P, PASSES, N // 4], I32, name="w4_sc", align_bytes=64, offset=W4_SCALES_AT)
         nc.vector.memset(w4_sc[:], 0)
 
-        tab_w = [keep.tile([P, T], I32, name="tab_w0", align_bytes=64), late.tile([P, T], I32, name="tab_w1", align_bytes=64, offset=4 * ROW)]
+        tab_w = [
+            keep.tile([P, T], I32, name="tab_w0", align_bytes=64),
+            placed.tile([P, T], I32, name="tab_w1", align_bytes=64, offset=WORDS_AT),
+        ]
         w_raw = {}
-        gates = [late.tile([P, T], F32, name=f"gates{i}", align_bytes=64, offset=(5 + i) * ROW) for i in range(8)]
+        gates = [placed.tile([P, T], F32, name=f"gates{i}", align_bytes=64, offset=GATES_AT + i * SLOT) for i in range(PLANES)]
 
         def load_w1(b, a):
-            if (b, a) == (0, 0):
-                raw = keep.tile([P, PACK, KP], F32, name="w_raw_first", align_bytes=64)
+            piece = PASSES * b + a
+            if piece == 0:
+                raw = keep.tile([P, PACK, SPAN], F32, name="w_raw_first", align_bytes=64)
             else:
-                raw = late.tile([P, PACK, KP], F32, name=f"w_raw{b}{a}", align_bytes=64, offset=(2 * b + a - 1) * ROW)
-            nc.sync.dma_start(out=raw[:], in_=w1[a * KP : (a + 1) * KP, b * KP : (b + 1) * KP].rearrange("(p j) c -> p j c", j=PACK))
+                raw = placed.tile([P, PACK, SPAN], F32, name=f"w_raw{b}{a}", align_bytes=64, offset=RAW_AT + (piece - 1) * SLOT)
+            rows = w1[a * SPAN : (a + 1) * SPAN, b * SPAN : (b + 1) * SPAN]
+            nc.sync.dma_start(out=raw[:], in_=rows.rearrange("(p j) c -> p j c", j=PACK))
             w_raw[b, a] = raw
 
         def load_words(a):
@@ -66,11 +90,12 @@ def tile_list_click_gated_features_kernel(tc, tab_words, tab_scales, offs, w1, b
 
         def load_gates(i):
             b, t = divmod(i, PACK)
-            nc.sync.dma_start(out=gates[i][:], in_=gT[b * KP : (b + 1) * KP, :].rearrange("(p t) c -> p t c", t=PACK)[:, t, :])
+            block = gT[b * SPAN : (b + 1) * SPAN, :].rearrange("(p t) c -> p t c", t=PACK)
+            nc.sync.dma_start(out=gates[i][:], in_=block[:, t, :])
 
-        b1_sb = late.tile([P, PASSES, 2 * PACK], F32, name="b1_sb", align_bytes=64, offset=13 * ROW + 1024)
-        b2_sb = late.tile([P, N // P, 8], F32, name="b2_sb", align_bytes=64, offset=13 * ROW + 1088)
-        w4_w = late.tile([P, PASSES, 2 * N // 4], I32, name="w4_w", align_bytes=64, offset=13 * ROW + 2048)
+        b1_sb = placed.tile([P, PASSES, PAD], F32, name="b1_sb", align_bytes=64, offset=B1_AT)
+        b2_sb = placed.tile([P, N // P, PAD], F32, name="b2_sb", align_bytes=64, offset=B2_AT)
+        w4_w = placed.tile([P, PASSES, 2 * N // 4], I32, name="w4_w", align_bytes=64, offset=W4_WORDS_AT)
 
         load_words(0)
         load_w1(0, 0)
@@ -78,15 +103,16 @@ def tile_list_click_gated_features_kernel(tc, tab_words, tab_scales, offs, w1, b
         nc.sync.dma_start(out=b1_sb[:, :, 0:PACK], in_=b1.rearrange("(b p t) -> p b t", b=PASSES, t=PACK))
         load_words(1)
         load_w1(1, 0)
-        load_w1(1, 1)
         load_gates(0)
         load_gates(1)
+        load_w1(1, 1)
         load_gates(2)
         load_gates(3)
-        for q in range(4):
-            nc.sync.dma_start(out=w4_sc[32 * q : 32 * q + 4, :, :], in_=w4_scales[:, 4 * q : 4 * q + 4, :].bitcast(I32).rearrange("a r c -> r a c"))
+        for q in range(QUADRANTS):
+            scale_rows = w4_scales[:, 4 * q : 4 * q + 4, :].bitcast(I32).rearrange("a r c -> r a c")
+            nc.sync.dma_start(out=w4_sc[32 * q : 32 * q + 4, :, :], in_=scale_rows)
         nc.sync.dma_start(out=w4_w[:, 0, :], in_=w4_words[0].bitcast(I32))
-        for i in range(4, 8):
+        for i in range(PACK, PLANES):
             load_gates(i)
         nc.sync.dma_start(out=w4_w[:, 1, :], in_=w4_words[1].bitcast(I32))
         with nc.allow_non_contiguous_dma(reason="one bias value to a partition"):
@@ -94,32 +120,39 @@ def tile_list_click_gated_features_kernel(tc, tab_words, tab_scales, offs, w1, b
 
         v_sc = keep.tile([P, S], U8, name="v_sc", align_bytes=64)
         v_w = [keep.tile([P, S], U32, name=f"v_w{a}", align_bytes=64) for a in range(PASSES)]
-        w_codes = keep.tile([P, PASSES, PASSES, KP], U32, name="w_codes", align_bytes=64)
-        w_sc = keep.tile([P, PASSES, PASSES, KP], U8, name="w_sc", align_bytes=64)
+        w_codes = keep.tile([P, PASSES, PASSES, SPAN], U32, name="w_codes", align_bytes=64)
+        w_sc = keep.tile([P, PASSES, PASSES, SPAN], U8, name="w_sc", align_bytes=64)
         w_bf = {}
 
-        def round_w1(b, a, t0, t1, on_vector):
-            if (b, a) not in w_bf:
-                w_bf[b, a] = stage.tile([P, PACK, P, PACK], BF16, name="w_bf", tag="w_bf", bufs=2, align_bytes=64)
-            dst = w_bf[b, a][:, t0:t1, :, :].rearrange("p t m j -> p m j t")
-            src = w_raw[b, a][:].rearrange("p j (m t) -> p m j t", t=PACK)[:, :, :, t0:t1]
+        def copy(dst, src, on_vector):
             if on_vector:
                 nc.vector.tensor_copy(out=dst, in_=src)
             else:
                 nc.scalar.copy(out=dst, in_=src)
 
+        def round_w1(b, a, t0, t1, on_vector):
+            if (b, a) == (1, 1) and t0 == 0:
+                w_bf[b, a] = placed.tile([P, PACK, P, PACK], BF16, name="w_bf_last", align_bytes=64, offset=SIG_AT)
+            if (b, a) not in w_bf:
+                w_bf[b, a] = ring.tile([P, PACK, P, PACK], BF16, name="w_bf", tag="w_bf", bufs=2, align_bytes=64)
+            dst = w_bf[b, a][:, t0:t1, :, :].rearrange("p t m j -> p m j t")
+            src = w_raw[b, a][:].rearrange("p j (m t) -> p m j t", t=PACK)[:, :, :, t0:t1]
+            copy(dst, src, on_vector)
+
         def quantize_w1(b, a):
-            nc.vector.quantize_mx(out=w_codes[:, b, a, :].bitcast(FP8X4), scales=w_sc[:, b, a, :], in_=w_bf[b, a][:].rearrange("p t m j -> p (t m j)"))
+            values = w_bf[b, a][:].rearrange("p t m j -> p (t m j)")
+            nc.vector.quantize_mx(out=w_codes[:, b, a, :].bitcast(FP8X4), scales=w_sc[:, b, a, :], in_=values)
 
         def gather_words(a, lo, hi):
             nc.vector.tensor_copy(v_w[a][:, lo:hi], tab_w[a][:].bitcast(U32).indirect(picks(lo, hi)))
 
-        sig = {}
+        sig_plane = {}
+        sig_half = {}
 
         def hidden(i, half):
             b, t = divmod(i, PACK)
             cols = slice(half * HALF, (half + 1) * HALF)
-            acc = psum.tile([P, HALF], F32, name="acc", tag="bank")
+            acc = psum.tile([P, HALF], F32, name=f"acc{i}_{half}", offset=((2 * i + half) % 4 + 4 * b) * BANK)
             for a in range(PASSES):
                 nc.tensor.matmul_mx(
                     out=acc[:],
@@ -130,14 +163,15 @@ def tile_list_click_gated_features_kernel(tc, tab_words, tab_scales, offs, w1, b
                     start=(a == 0),
                     stop=(a == PASSES - 1),
                 )
-            at = SIG_AT + (i % 6) * 4096
-            if i >= 6:
-                sig[i, half] = late.tile([P, HALF], F32, name=f"sig{i}_{half}", align_bytes=64, offset=at + half * 2048)[:]
+            at = SIG_AT + (i % SIG_SLOTS) * SIG_BYTES
+            if i >= SIG_SLOTS:
+                tile = placed.tile([P, HALF], F32, name=f"sig{i}_{half}", align_bytes=64, offset=at + half * SIG_BYTES // 2)
+                sig_half[i, half] = tile[:]
             else:
                 if half == 0:
-                    sig[i] = late.tile([P, S], F32, name=f"sig{i}", align_bytes=64, offset=at)
-                sig[i, half] = sig[i][:, cols]
-            nc.scalar.activation(out=sig[i, half], in_=acc[:], func=ACT.Sigmoid, bias=b1_sb[:, b, t : t + 1])
+                    sig_plane[i] = placed.tile([P, S], F32, name=f"sig{i}", align_bytes=64, offset=at)
+                sig_half[i, half] = sig_plane[i][:, cols]
+            nc.scalar.activation(out=sig_half[i, half], in_=acc[:], func=ACT.Sigmoid, bias=b1_sb[:, b, t : t + 1])
 
         h32 = [keep.tile([P, PACK, S], F32, name=f"h32_{b}", align_bytes=64) for b in range(PASSES)]
         h_bf = [keep.tile([P, S, PACK], BF16, name=f"h_bf{b}", align_bytes=64) for b in range(PASSES)]
@@ -146,25 +180,28 @@ def tile_list_click_gated_features_kernel(tc, tab_words, tab_scales, offs, w1, b
 
         def gate(i, lo, hi):
             b, t = divmod(i, PACK)
-            nc.vector.tensor_tensor(h32[b][:, t, lo:hi], gates[i][:].indirect(picks(lo, hi)), sig[i, lo // HALF][:, lo % HALF : lo % HALF + hi - lo] if i >= 6 else sig[i][:, lo:hi], ALU.mult)
+            if i >= SIG_SLOTS:
+                values = sig_half[i, lo // HALF][:, lo % HALF : lo % HALF + hi - lo]
+            else:
+                values = sig_plane[i][:, lo:hi]
+            nc.vector.tensor_tensor(h32[b][:, t, lo:hi], gates[i][:].indirect(picks(lo, hi)), values, ALU.mult)
 
         def round_h(b, lo, hi, on_vector, t0=0, t1=PACK):
             dst = h_bf[b][:, lo:hi, t0:t1].rearrange("p (c i) t -> p c t i", i=4)
             src = h32[b][:, t0:t1, lo:hi].rearrange("p t (c i) -> p c t i", i=4)
-            if on_vector:
-                nc.vector.tensor_copy(out=dst, in_=src)
-            else:
-                nc.scalar.copy(out=dst, in_=src)
+            copy(dst, src, on_vector)
 
         def quantize_h(b, lo, hi):
             half = lo // HALF
             if (b, half) not in h_codes:
+                name = f"h_codes{b}{half}"
                 if b == 0:
-                    h_codes[b, half] = late.tile([P, HALF], U32, name=f"h_codes{b}{half}", align_bytes=64, offset=SIG_AT + half * 4096)
+                    h_codes[b, half] = placed.tile([P, HALF], U32, name=name, align_bytes=64, offset=SIG_AT + half * SIG_BYTES)
                 else:
-                    h_codes[b, half] = keep.tile([P, HALF], U32, name=f"h_codes{b}{half}", align_bytes=64)
+                    h_codes[b, half] = keep.tile([P, HALF], U32, name=name, align_bytes=64)
             codes = h_codes[b, half][:, lo - half * HALF : hi - half * HALF]
-            nc.vector.quantize_mx(out=codes.bitcast(FP8X4), scales=h_sc[:, b, lo:hi], in_=h_bf[b][:, lo:hi, :].rearrange("p s t -> p (s t)"))
+            values = h_bf[b][:, lo:hi, :].rearrange("p s t -> p (s t)")
+            nc.vector.quantize_mx(out=codes.bitcast(FP8X4), scales=h_sc[:, b, lo:hi], in_=values)
 
         sums = {}
 
@@ -172,7 +209,7 @@ def tile_list_click_gated_features_kernel(tc, tab_words, tab_scales, offs, w1, b
             cols = slice(half * HALF, (half + 1) * HALF)
             for c in range(N // P):
                 if b == 0:
-                    sums[c, half] = psum.tile([P, HALF], F32, name="total", tag="bank")
+                    sums[c, half] = psum.tile([P, HALF], F32, name=f"total{c}_{half}", offset=(4 * half + c) * BANK)
                 nc.tensor.matmul_mx(
                     out=sums[c, half][:],
                     lhsT=w4_w[:, b, :].bitcast(U8)[:, 2 * c * P : 2 * (c + 1) * P].bitcast(FP4X4),
@@ -187,7 +224,7 @@ def tile_list_click_gated_features_kernel(tc, tab_words, tab_scales, offs, w1, b
 
         def finish(c, half, on_vector):
             if half not in results:
-                results[half] = late.tile([P, PACK, KP], F32, name=f"result{half}", align_bytes=64, offset=(3 * (1 - half)) * ROW)
+                results[half] = placed.tile([P, N // P, HALF], F32, name=f"result{half}", align_bytes=64, offset=RESULT_AT[half])
             dst = results[half][:, c, :]
             if on_vector:
                 nc.vector.tensor_scalar(out=dst, in0=sums[c, half][:], scalar1=b2_sb[:, c, 0:1], scalar2=None, op0=ALU.add)
@@ -207,48 +244,52 @@ def tile_list_click_gated_features_kernel(tc, tab_words, tab_scales, offs, w1, b
         round_w1(1, 0, 0, 2, True)
         round_w1(1, 0, 2, 4, True)
         quantize_w1(1, 0)
-        round_w1(1, 1, 0, 2, True)
-        round_w1(1, 1, 2, 4, True)
-        quantize_w1(1, 1)
-        for i in range(4):
+
+        for i in range(PACK):
             hidden(i, 0)
             hidden(i, 1)
-        gate(0, 0, S)
+        gate(0, 0, HALF)
+        gate(0, HALF, S)
         gate(1, 0, S)
+        round_w1(1, 1, 0, 2, False)
+        round_w1(1, 1, 2, 4, True)
+        quantize_w1(1, 1)
         gate(2, 0, S)
-        hidden(4, 0)
-        hidden(4, 1)
+        for i in range(PACK, SIG_SLOTS):
+            hidden(i, 0)
+            hidden(i, 1)
         gate(3, 0, HALF)
         gate(3, HALF, S)
         round_h(0, 0, HALF, False)
         gate(4, 0, S)
-        hidden(5, 0)
-        hidden(5, 1)
-        round_h(0, HALF, S, False)
         gate(5, 0, S)
-        for i in range(6, 8):
+        for i in range(SIG_SLOTS, PLANES):
             hidden(i, 0)
             hidden(i, 1)
+        round_h(0, HALF, S, False)
         round_h(1, 0, HALF, False, 0, 2)
         gate(6, 0, HALF)
         gate(6, HALF, S)
         quantize_h(0, 0, HALF)
         project(0, 0)
-        for lo in range(0, HALF, 128):
-            gate(7, lo, lo + 128)
-            round_h(1, lo, lo + 128, False, 2, 4)
-            if lo % 256 == 128:
-                quantize_h(1, lo - 128, lo + 128)
+
+        last = PLANES - 1
+        for lo in range(0, HALF, CHUNK):
+            gate(last, lo, lo + CHUNK)
+            round_h(1, lo, lo + CHUNK, lo + CHUNK == HALF, 2, 4)
+            if (lo + CHUNK) % QUARTER == 0:
+                quantize_h(1, lo + CHUNK - QUARTER, lo + CHUNK)
         project(1, 0)
-        gate(7, 512, 640)
-        gate(7, 640, 768)
-        round_h(1, HALF, 768, False)
-        gate(7, 768, S)
-        round_h(1, 768, S, True)
+        gate(last, HALF, HALF + CHUNK)
+        gate(last, HALF + CHUNK, HALF + QUARTER)
+        round_h(1, HALF, HALF + QUARTER, False)
+        gate(last, HALF + QUARTER, S)
+        round_h(1, HALF + QUARTER, S, True)
         quantize_h(0, HALF, S)
         project(0, 1)
         quantize_h(1, HALF, S)
         project(1, 1)
+
         for c in range(N // P):
             finish(c, 0, False)
         for c in range(N // P):

@@ -59,12 +59,6 @@ def tile_list_click_gated_features_kernel(tc, tab_words, tab_scales, offs, w1, b
 
         tab_sc = keep.tile([P, T // 4], I32, name="tab_sc", align_bytes=64)
         nc.vector.memset(tab_sc[:], 0)
-        for q in range(QUADRANTS):
-            nc.scalar.dma_start(out=tab_sc[32 * q : 32 * q + 8, :], in_=tab_scales[:, 4 * q : 4 * q + 4, :].bitcast(I32))
-
-        warm = placed.tile([P, HELD_BYTES // 4], F32, name="warm", offset=0, align_bytes=64)
-        nc.vector.memset(warm[:, 0:1], 0.0)
-        nc.scalar.activation(out=warm[:, 1:2], in_=warm[:, 0:1], func=ACT.Sigmoid)
         w4_sc = placed.tile([P, PASSES, N // 4], I32, name="w4_sc", align_bytes=64, offset=W4_SCALES_AT)
         nc.vector.memset(w4_sc[:], 0)
 
@@ -98,6 +92,8 @@ def tile_list_click_gated_features_kernel(tc, tab_words, tab_scales, offs, w1, b
         w4_w = placed.tile([P, PASSES, 2 * N // 4], I32, name="w4_w", align_bytes=64, offset=W4_WORDS_AT)
 
         load_words(0)
+        for q in range(QUADRANTS):
+            nc.sync.dma_start(out=tab_sc[32 * q : 32 * q + 8, :], in_=tab_scales[:, 4 * q : 4 * q + 4, :].bitcast(I32))
         load_w1(0, 0)
         load_w1(0, 1)
         nc.sync.dma_start(out=b1_sb[:, :, 0:PACK], in_=b1.rearrange("(b p t) -> p b t", b=PASSES, t=PACK))
@@ -196,7 +192,7 @@ def tile_list_click_gated_features_kernel(tc, tab_words, tab_scales, offs, w1, b
             if (b, half) not in h_codes:
                 name = f"h_codes{b}{half}"
                 if b == 0:
-                    h_codes[b, half] = placed.tile([P, HALF], U32, name=name, align_bytes=64, offset=SIG_AT + half * SIG_BYTES)
+                    h_codes[b, half] = placed.tile([P, HALF], U32, name=name, align_bytes=64, offset=SIG_AT + half * (SIG_BYTES + SIG_BYTES // 2))
                 else:
                     h_codes[b, half] = keep.tile([P, HALF], U32, name=name, align_bytes=64)
             codes = h_codes[b, half][:, lo - half * HALF : hi - half * HALF]
@@ -284,10 +280,11 @@ def tile_list_click_gated_features_kernel(tc, tab_words, tab_scales, offs, w1, b
         gate(last, HALF + CHUNK, HALF + QUARTER)
         round_h(1, HALF, HALF + QUARTER, False)
         gate(last, HALF + QUARTER, S)
-        round_h(1, HALF + QUARTER, S, True)
         quantize_h(0, HALF, S)
         project(0, 1)
-        quantize_h(1, HALF, S)
+        round_h(1, HALF + QUARTER, S, True)
+        quantize_h(1, HALF, HALF + QUARTER)
+        quantize_h(1, HALF + QUARTER, S)
         project(1, 1)
 
         for c in range(N // P):

@@ -216,17 +216,51 @@ def tile_list_click_gated_features_kernel(tc, tab_words, tab_scales, offs, w1, b
                     stop=(b == PASSES - 1),
                 )
 
+        banks = {}
+
+        def project_quarter(b, q):
+            for pair in range(2):
+                if b == 0:
+                    banks[q, pair] = psum.tile([P, 2, QUARTER], F32, name=f"bank{q}_{pair}", offset=(2 * q + pair) * BANK)
+                for k in range(2):
+                    c = 2 * pair + k
+                    for n in range(2):
+                        cols = slice(q * QUARTER + n * P, q * QUARTER + (n + 1) * P)
+                        nc.tensor.matmul_mx(
+                            out=banks[q, pair][:, k, n * P : (n + 1) * P],
+                            lhsT=w4_w[:, b, :].bitcast(U8)[:, 2 * c * P : 2 * (c + 1) * P].bitcast(FP4X4),
+                            lhsT_scale=w4_sc[:, b, :].bitcast(U8)[:, c * P : (c + 1) * P],
+                            rhs=h_codes[b, 0][:, cols].bitcast(FP8X4),
+                            rhs_scale=h_sc[:, b, cols],
+                            start=(b == 0 and k == 0 and n == 0),
+                            stop=(b == PASSES - 1 and k == 1 and n == 1),
+                        )
+
+        def finish_quarter(q, pair):
+            dst = placed.tile([P, 2, QUARTER], F32, name=f"result_q{q}_{pair}", align_bytes=64, offset=RESULT_AT[0] + BANK * (2 * q + pair))
+            for k in range(2):
+                nc.scalar.activation(out=dst[:, k, :], in_=banks[q, pair][:, k, :], func=ACT.Identity, bias=b2_sb[:, 2 * pair + k, 0:1])
+            rows = out[2 * pair * P : 2 * (pair + 1) * P, q * QUARTER : (q + 1) * QUARTER].rearrange("(k p) j -> p k j", p=P)
+            if (q, pair) == (0, 0):
+                for k in range(2):
+                    nc.sync.dma_start(out=rows[:, k, :], in_=dst[:, k, :])
+            else:
+                nc.sync.dma_start(out=rows, in_=dst[:])
+
         results = {}
 
         def finish(c, half, on_vector):
             if half not in results:
                 results[half] = placed.tile([P, N // P, HALF], F32, name=f"result{half}", align_bytes=64, offset=RESULT_AT[half])
-            dst = results[half][:, c, :]
-            if on_vector:
-                nc.vector.tensor_scalar(out=dst, in0=sums[c, half][:], scalar1=b2_sb[:, c, 0:1], scalar2=None, op0=ALU.add)
-            else:
-                nc.scalar.activation(out=dst, in_=sums[c, half][:], func=ACT.Identity, bias=b2_sb[:, c, 0:1])
-            nc.sync.dma_start(out=out[c * P : (c + 1) * P, half * HALF : (half + 1) * HALF], in_=dst)
+            width = HALF if c < 2 else QUARTER
+            for lo in range(0, HALF, width):
+                dst = results[half][:, c, lo : lo + width]
+                src = sums[c, half][:, lo : lo + width]
+                if on_vector:
+                    nc.vector.tensor_scalar(out=dst, in0=src, scalar1=b2_sb[:, c, 0:1], scalar2=None, op0=ALU.add)
+                else:
+                    nc.scalar.activation(out=dst, in_=src, func=ACT.Identity, bias=b2_sb[:, c, 0:1])
+                nc.sync.dma_start(out=out[c * P : (c + 1) * P, half * HALF + lo : half * HALF + lo + width], in_=dst)
 
         gather_words(0, 0, S)
         nc.vector.tensor_copy(v_sc[:], tab_sc[:].bitcast(U8).indirect(offsets[:]))
@@ -264,10 +298,12 @@ def tile_list_click_gated_features_kernel(tc, tab_words, tab_scales, offs, w1, b
             hidden(i, 1)
         round_h(0, HALF, S, False)
         round_h(1, 0, HALF, False, 0, 2)
+        round_h(1, HALF, S, False, 0, 2)
         gate(6, 0, HALF)
         gate(6, HALF, S)
         quantize_h(0, 0, HALF)
-        project(0, 0)
+        project_quarter(0, 0)
+        project_quarter(0, 1)
 
         last = PLANES - 1
         for lo in range(0, HALF, CHUNK):
@@ -275,19 +311,20 @@ def tile_list_click_gated_features_kernel(tc, tab_words, tab_scales, offs, w1, b
             round_h(1, lo, lo + CHUNK, lo + CHUNK == HALF, 2, 4)
             if (lo + CHUNK) % QUARTER == 0:
                 quantize_h(1, lo + CHUNK - QUARTER, lo + CHUNK)
-        project(1, 0)
+                project_quarter(1, lo // QUARTER)
         gate(last, HALF, HALF + CHUNK)
         gate(last, HALF + CHUNK, HALF + QUARTER)
-        round_h(1, HALF, HALF + QUARTER, False)
+        round_h(1, HALF, HALF + QUARTER, False, 2, 4)
         gate(last, HALF + QUARTER, S)
         quantize_h(0, HALF, S)
         project(0, 1)
-        round_h(1, HALF + QUARTER, S, True)
+        round_h(1, HALF + QUARTER, S, True, 2, 4)
         quantize_h(1, HALF, HALF + QUARTER)
         quantize_h(1, HALF + QUARTER, S)
         project(1, 1)
 
+        for q in range(2):
+            for pair in range(2):
+                finish_quarter(q, pair)
         for c in range(N // P):
-            finish(c, 0, False)
-        for c in range(N // P):
-            finish(c, 1, c != 2)
+            finish(c, 1, c % 2 == 0)

@@ -40,7 +40,7 @@ W4_WORDS_AT = W4_SCALES_AT + 2048
 HELD_BYTES = W4_WORDS_AT + 2048
 SIG_AT = HELD_BYTES
 SIG_BYTES = 4 * S
-SIG_SLOTS = 6
+SPLIT_FROM = 6
 
 
 def tile_list_click_gated_features_kernel(tc, tab_words, tab_scales, offs, w1, b1, gT, w4_words, w4_scales, b2, out):
@@ -100,16 +100,16 @@ def tile_list_click_gated_features_kernel(tc, tab_words, tab_scales, offs, w1, b
         load_words(1)
         load_w1(1, 0)
         load_gates(0)
-        load_gates(1)
         load_w1(1, 1)
+        load_gates(1)
         load_gates(2)
-        load_gates(3)
+        for i in range(3, PLANES - 1):
+            load_gates(i)
         for q in range(QUADRANTS):
             scale_rows = w4_scales[:, 4 * q : 4 * q + 4, :].bitcast(I32).rearrange("a r c -> r a c")
             nc.sync.dma_start(out=w4_sc[32 * q : 32 * q + 4, :, :], in_=scale_rows)
         nc.sync.dma_start(out=w4_w[:, 0, :], in_=w4_words[0].bitcast(I32))
-        for i in range(PACK, PLANES):
-            load_gates(i)
+        load_gates(PLANES - 1)
         nc.sync.dma_start(out=w4_w[:, 1, :], in_=w4_words[1].bitcast(I32))
         with nc.allow_non_contiguous_dma(reason="one bias value to a partition"):
             nc.sync.dma_start(out=b2_sb[:, :, 0], in_=b2.rearrange("(c p) -> p c", p=P))
@@ -127,17 +127,16 @@ def tile_list_click_gated_features_kernel(tc, tab_words, tab_scales, offs, w1, b
                 nc.scalar.copy(out=dst, in_=src)
 
         def round_w1(b, a, t0, t1, on_vector):
-            if (b, a) == (1, 1) and t0 == 0:
-                w_bf[b, a] = placed.tile([P, PACK, P, PACK], BF16, name="w_bf_last", align_bytes=64, offset=SIG_AT)
             if (b, a) not in w_bf:
                 w_bf[b, a] = ring.tile([P, PACK, P, PACK], BF16, name="w_bf", tag="w_bf", bufs=2, align_bytes=64)
             dst = w_bf[b, a][:, t0:t1, :, :].rearrange("p t m j -> p m j t")
             src = w_raw[b, a][:].rearrange("p j (m t) -> p m j t", t=PACK)[:, :, :, t0:t1]
             copy(dst, src, on_vector)
 
-        def quantize_w1(b, a):
-            values = w_bf[b, a][:].rearrange("p t m j -> p (t m j)")
-            nc.vector.quantize_mx(out=w_codes[:, b, a, :].bitcast(FP8X4), scales=w_sc[:, b, a, :], in_=values)
+        def quantize_w1(b, a, t0=0, t1=PACK):
+            values = w_bf[b, a][:, t0:t1, :, :].rearrange("p t m j -> p (t m j)")
+            cols = slice(t0 * P, t1 * P)
+            nc.vector.quantize_mx(out=w_codes[:, b, a, cols].bitcast(FP8X4), scales=w_sc[:, b, a, cols], in_=values)
 
         def gather_words(a, lo, hi):
             nc.vector.tensor_copy(v_w[a][:, lo:hi], tab_w[a][:].bitcast(U32).indirect(picks(lo, hi)))
@@ -159,8 +158,8 @@ def tile_list_click_gated_features_kernel(tc, tab_words, tab_scales, offs, w1, b
                     start=(a == 0),
                     stop=(a == PASSES - 1),
                 )
-            at = SIG_AT + (i % SIG_SLOTS) * SIG_BYTES
-            if i >= SIG_SLOTS:
+            at = RAW_AT + 2 * SLOT if i == PACK - 1 else SIG_AT + i * SIG_BYTES
+            if i >= SPLIT_FROM:
                 tile = placed.tile([P, HALF], F32, name=f"sig{i}_{half}", align_bytes=64, offset=at + half * SIG_BYTES // 2)
                 sig_half[i, half] = tile[:]
             else:
@@ -170,13 +169,16 @@ def tile_list_click_gated_features_kernel(tc, tab_words, tab_scales, offs, w1, b
             nc.scalar.activation(out=sig_half[i, half], in_=acc[:], func=ACT.Sigmoid, bias=b1_sb[:, b, t : t + 1])
 
         h32 = [keep.tile([P, PACK, S], F32, name=f"h32_{b}", align_bytes=64) for b in range(PASSES)]
-        h_bf = [keep.tile([P, S, PACK], BF16, name=f"h_bf{b}", align_bytes=64) for b in range(PASSES)]
+        h_bf = [
+            placed.tile([P, S, PACK], BF16, name="h_bf0", align_bytes=64, offset=RAW_AT),
+            keep.tile([P, S, PACK], BF16, name="h_bf1", align_bytes=64),
+        ]
         h_codes = {}
         h_sc = keep.tile([P, PASSES, S], U8, name="h_sc", align_bytes=64)
 
         def gate(i, lo, hi):
             b, t = divmod(i, PACK)
-            if i >= SIG_SLOTS:
+            if i >= SPLIT_FROM:
                 values = sig_half[i, lo // HALF][:, lo % HALF : lo % HALF + hi - lo]
             else:
                 values = sig_plane[i][:, lo:hi]
@@ -192,7 +194,7 @@ def tile_list_click_gated_features_kernel(tc, tab_words, tab_scales, offs, w1, b
             if (b, half) not in h_codes:
                 name = f"h_codes{b}{half}"
                 if b == 0:
-                    h_codes[b, half] = placed.tile([P, HALF], U32, name=name, align_bytes=64, offset=SIG_AT + half * (SIG_BYTES + SIG_BYTES // 2))
+                    h_codes[b, half] = placed.tile([P, HALF], U32, name=name, align_bytes=64, offset=SIG_AT + SPLIT_FROM * SIG_BYTES + half * (SIG_BYTES + SIG_BYTES // 2))
                 else:
                     h_codes[b, half] = keep.tile([P, HALF], U32, name=name, align_bytes=64)
             codes = h_codes[b, half][:, lo - half * HALF : hi - half * HALF]
@@ -275,27 +277,27 @@ def tile_list_click_gated_features_kernel(tc, tab_words, tab_scales, offs, w1, b
         round_w1(1, 0, 2, 4, True)
         quantize_w1(1, 0)
 
-        for i in range(PACK):
+        for i in range(PACK - 1):
             hidden(i, 0)
             hidden(i, 1)
-        gate(0, 0, HALF)
-        gate(0, HALF, S)
-        gate(1, 0, S)
+        gate(0, 0, S)
         round_w1(1, 1, 0, 2, False)
         round_w1(1, 1, 2, 4, True)
-        quantize_w1(1, 1)
+        quantize_w1(1, 1, 2, 4)
+        quantize_w1(1, 1, 0, 2)
+        hidden(PACK - 1, 0)
+        hidden(PACK - 1, 1)
+        gate(1, 0, S)
         gate(2, 0, S)
-        for i in range(PACK, SIG_SLOTS):
+        for i in range(PACK, PLANES):
             hidden(i, 0)
             hidden(i, 1)
         gate(3, 0, HALF)
         gate(3, HALF, S)
         round_h(0, 0, HALF, False)
         gate(4, 0, S)
-        gate(5, 0, S)
-        for i in range(SIG_SLOTS, PLANES):
-            hidden(i, 0)
-            hidden(i, 1)
+        gate(5, 0, HALF)
+        gate(5, HALF, S)
         round_h(0, HALF, S, False)
         round_h(1, 0, HALF, False, 0, 2)
         round_h(1, HALF, S, False, 0, 2)
@@ -306,14 +308,13 @@ def tile_list_click_gated_features_kernel(tc, tab_words, tab_scales, offs, w1, b
         project_quarter(0, 1)
 
         last = PLANES - 1
-        for lo in range(0, HALF, CHUNK):
-            gate(last, lo, lo + CHUNK)
-            round_h(1, lo, lo + CHUNK, lo + CHUNK == HALF, 2, 4)
-            if (lo + CHUNK) % QUARTER == 0:
-                quantize_h(1, lo + CHUNK - QUARTER, lo + CHUNK)
+        for lo, hi in ((0, CHUNK), (CHUNK, QUARTER), (QUARTER, HALF)):
+            gate(last, lo, hi)
+            round_h(1, lo, hi, False, 2, 4)
+            if hi % QUARTER == 0:
+                quantize_h(1, hi - QUARTER, hi)
                 project_quarter(1, lo // QUARTER)
-        gate(last, HALF, HALF + CHUNK)
-        gate(last, HALF + CHUNK, HALF + QUARTER)
+        gate(last, HALF, HALF + QUARTER)
         round_h(1, HALF, HALF + QUARTER, False, 2, 4)
         gate(last, HALF + QUARTER, S)
         quantize_h(0, HALF, S)

@@ -168,11 +168,25 @@ def tile_list_click_gated_features_kernel(tc, tab_words, tab_scales, offs, w1, b
                 sig_half[i, half] = sig_plane[i][:, cols]
             nc.scalar.activation(out=sig_half[i, half], in_=acc[:], func=ACT.Sigmoid, bias=b1_sb[:, b, t : t + 1])
 
-        h32 = [keep.tile([P, PACK, S], F32, name=f"h32_{b}", align_bytes=64) for b in range(PASSES)]
+        shared = keep.tile([P, PACK * S + 3 * QUARTER], F32, name="shared", align_bytes=64)
+        h32 = [
+            keep.tile([P, PACK, S], F32, name="h32_0", align_bytes=64),
+            shared[:, 0 : PACK * S].rearrange("p (t s) -> p t s", t=PACK),
+        ]
         h_bf = [
             placed.tile([P, S, PACK], BF16, name="h_bf0", align_bytes=64, offset=RAW_AT),
-            keep.tile([P, S, PACK], BF16, name="h_bf1", align_bytes=64),
         ]
+        late = {
+            0: shared[:, PACK * S - QUARTER : PACK * S + 3 * QUARTER].bitcast(BF16).rearrange("p (j t) -> p j t", t=PACK),
+            HALF: keep.tile([P, HALF, PACK], BF16, name="late_second", align_bytes=64),
+        }
+
+        def rounded(b, lo, hi):
+            if b == 0:
+                return h_bf[0][:, lo:hi, :]
+            base = lo // HALF * HALF
+            return late[base][:, lo - base : hi - base, :]
+
         h_codes = {}
         h_sc = keep.tile([P, PASSES, S], U8, name="h_sc", align_bytes=64)
 
@@ -185,7 +199,7 @@ def tile_list_click_gated_features_kernel(tc, tab_words, tab_scales, offs, w1, b
             nc.vector.tensor_tensor(h32[b][:, t, lo:hi], gates[i][:].indirect(picks(lo, hi)), values, ALU.mult)
 
         def round_h(b, lo, hi, on_vector, t0=0, t1=PACK):
-            dst = h_bf[b][:, lo:hi, t0:t1].rearrange("p (c i) t -> p c t i", i=4)
+            dst = rounded(b, lo, hi)[:, :, t0:t1].rearrange("p (c i) t -> p c t i", i=4)
             src = h32[b][:, t0:t1, lo:hi].rearrange("p t (c i) -> p c t i", i=4)
             copy(dst, src, on_vector)
 
@@ -198,7 +212,7 @@ def tile_list_click_gated_features_kernel(tc, tab_words, tab_scales, offs, w1, b
                 else:
                     h_codes[b, half] = keep.tile([P, HALF], U32, name=name, align_bytes=64)
             codes = h_codes[b, half][:, lo - half * HALF : hi - half * HALF]
-            values = h_bf[b][:, lo:hi, :].rearrange("p s t -> p (s t)")
+            values = rounded(b, lo, hi).rearrange("p s t -> p (s t)")
             nc.vector.quantize_mx(out=codes.bitcast(FP8X4), scales=h_sc[:, b, lo:hi], in_=values)
 
         sums = {}
@@ -275,7 +289,8 @@ def tile_list_click_gated_features_kernel(tc, tab_words, tab_scales, offs, w1, b
         gather_words(1, HALF, S)
         round_w1(1, 0, 0, 2, True)
         round_w1(1, 0, 2, 4, True)
-        quantize_w1(1, 0)
+        quantize_w1(1, 0, 0, 2)
+        quantize_w1(1, 0, 2, 4)
 
         for i in range(PACK - 1):
             hidden(i, 0)

@@ -199,8 +199,12 @@ def tile_list_click_gated_features_kernel(tc, tab_words, tab_scales, offs, w1, b
             nc.vector.tensor_tensor(h32[b][:, t, lo:hi], gates[i][:].indirect(picks(lo, hi)), values, ALU.mult)
 
         def round_h(b, lo, hi, on_vector, t0=0, t1=PACK):
-            dst = rounded(b, lo, hi)[:, :, t0:t1].rearrange("p (c i) t -> p c t i", i=4)
-            src = h32[b][:, t0:t1, lo:hi].rearrange("p t (c i) -> p c t i", i=4)
+            if t1 - t0 == PACK:
+                dst = rounded(b, lo, hi).rearrange("p (c i) t -> p c t i", i=4)
+                src = h32[b][:, :, lo:hi].rearrange("p t (c i) -> p c t i", i=4)
+            else:
+                dst = rounded(b, lo, hi)[:, :, t0:t1]
+                src = h32[b][:, t0:t1, lo:hi].rearrange("p t j -> p j t")
             copy(dst, src, on_vector)
 
         def quantize_h(b, lo, hi):

from contextlib import ExitStack

import concourse.mybir as mybir

K, T, S, H, N = 1024, 2048, 1024, 1024, 512
FLOPS = 2 * K * H * S + 2 * H * N * S

F32 = mybir.dt.float32
BF16 = mybir.dt.bfloat16
I32 = mybir.dt.int32
U32 = mybir.dt.uint32
U16 = mybir.dt.uint16
U8 = mybir.dt.uint8
FP8X4 = mybir.dt.float8_e4m3fn_x4
FP4X4 = mybir.dt.float4_e2m1fn_x4
ACT = mybir.ActivationFunctionType
ALU = mybir.AluOpType

P = 128
PACK = 4
SPAN = P * PACK
PASSES = 2
PLANES = PASSES * PACK
QUADRANTS = 4
HALF = S // 2
QUARTER = S // 4
CHUNK = S // 8
BANK = 2048
PAD = 8

SLOT = 8192
RAW_AT = 0
RESULT_AT = (3 * SLOT, RAW_AT)
WORDS_AT = 4 * SLOT
GATES_AT = 5 * SLOT
W4_SCALES_AT = GATES_AT + PLANES * SLOT
B1_AT = W4_SCALES_AT + 1024
B2_AT = B1_AT + 64
W4_WORDS_AT = W4_SCALES_AT + 2048
HELD_BYTES = W4_WORDS_AT + 2048
SIG_AT = HELD_BYTES
SIG_BYTES = 4 * S
SPLIT_FROM = 6


def tile_list_click_gated_features_kernel(tc, tab_words, tab_scales, offs, w1, b1, gT, w4_words, w4_scales, b2, out):
    nc = tc.nc
    with ExitStack() as ctx:
        keep = ctx.enter_context(tc.tile_pool(name="keep", bufs=1))
        ring = ctx.enter_context(tc.tile_pool(name="ring", bufs=1))
        placed = ctx.enter_context(tc.tile_pool(name="placed", bufs=1))
        psum = ctx.enter_context(tc.psum_pool(name="psum", bufs=1))

        offsets = keep.tile([P, S // 16], U16, name="offsets")
        nc.sync.dma_start(offsets[:], offs)

        def picks(lo, hi):
            return offsets[:, lo // 16 : hi // 16]

        tab_sc = keep.tile([P, T // 4], I32, name="tab_sc", align_bytes=64)
        nc.vector.memset(tab_sc[:], 0)
        w4_sc = placed.tile([P, PASSES, N // 4], I32, name="w4_sc", align_bytes=64, offset=W4_SCALES_AT)
        nc.vector.memset(w4_sc[:], 0)

        tab_w = [
            keep.tile([P, T], I32, name="tab_w0", align_bytes=64),
            placed.tile([P, T], I32, name="tab_w1", align_bytes=64, offset=WORDS_AT),
        ]
        w_raw = {}
        gates = [placed.tile([P, T], F32, name=f"gates{i}", align_bytes=64, offset=GATES_AT + i * SLOT) for i in range(PLANES)]

        def load_w1(b, a):
            piece = PASSES * b + a
            if piece == 0:
                raw = keep.tile([P, PACK, SPAN], F32, name="w_raw_first", align_bytes=64)
            else:
                raw = placed.tile([P, PACK, SPAN], F32, name=f"w_raw{b}{a}", align_bytes=64, offset=RAW_AT + (piece - 1) * SLOT)
            rows = w1[a * SPAN : (a + 1) * SPAN, b * SPAN : (b + 1) * SPAN]
            nc.sync.dma_start(out=raw[:], in_=rows.rearrange("(p j) c -> p j c", j=PACK))
            w_raw[b, a] = raw

        def load_words(a):
            nc.sync.dma_start(out=tab_w[a][:], in_=tab_words[a].rearrange("p t i -> p (t i)").bitcast(I32))

        def load_gates(i):
            b, t = divmod(i, PACK)
            block = gT[b * SPAN : (b + 1) * SPAN, :].rearrange("(p t) c -> p t c", t=PACK)
            nc.sync.dma_start(out=gates[i][:], in_=block[:, t, :])

        b1_sb = placed.tile([P, PASSES, PAD], F32, name="b1_sb", align_bytes=64, offset=B1_AT)
        b2_sb = placed.tile([P, N // P, PAD], F32, name="b2_sb", align_bytes=64, offset=B2_AT)
        w4_w = placed.tile([P, PASSES, 2 * N // 4], I32, name="w4_w", align_bytes=64, offset=W4_WORDS_AT)

        load_words(0)
        for q in range(QUADRANTS):
            nc.sync.dma_start(out=tab_sc[32 * q : 32 * q + 8, :], in_=tab_scales[:, 4 * q : 4 * q + 4, :].bitcast(I32))
        load_w1(0, 0)
        load_w1(0, 1)
        nc.sync.dma_start(out=b1_sb[:, :, 0:PACK], in_=b1.rearrange("(b p t) -> p b t", b=PASSES, t=PACK))
        load_words(1)
        load_w1(1, 0)
        load_gates(0)
        load_w1(1, 1)
        load_gates(1)
        load_gates(2)
        for i in range(3, PLANES - 1):
            load_gates(i)
        for q in range(QUADRANTS):
            scale_rows = w4_scales[:, 4 * q : 4 * q + 4, :].bitcast(I32).rearrange("a r c -> r a c")
            nc.sync.dma_start(out=w4_sc[32 * q : 32 * q + 4, :, :], in_=scale_rows)
        nc.sync.dma_start(out=w4_w[:, 0, :], in_=w4_words[0].bitcast(I32))
        load_gates(PLANES - 1)
        nc.sync.dma_start(out=w4_w[:, 1, :], in_=w4_words[1].bitcast(I32))
        with nc.allow_non_contiguous_dma(reason="one bias value to a partition"):
            nc.sync.dma_start(out=b2_sb[:, :, 0], in_=b2.rearrange("(c p) -> p c", p=P))

        v_sc = keep.tile([P, S], U8, name="v_sc", align_bytes=64)
        v_w = [keep.tile([P, S], U32, name=f"v_w{a}", align_bytes=64) for a in range(PASSES)]
        w_codes = keep.tile([P, PASSES, PASSES, SPAN], U32, name="w_codes", align_bytes=64)
        w_sc = keep.tile([P, PASSES, PASSES, SPAN], U8, name="w_sc", align_bytes=64)
        w_bf = {}

        def copy(dst, src, on_vector):
            if on_vector:
                nc.vector.tensor_copy(out=dst, in_=src)
            else:
                nc.scalar.copy(out=dst, in_=src)

        def round_w1(b, a, t0, t1, on_vector):
            if (b, a) not in w_bf:
                w_bf[b, a] = ring.tile([P, PACK, P, PACK], BF16, name="w_bf", tag="w_bf", bufs=2, align_bytes=64)
            dst = w_bf[b, a][:, t0:t1, :, :].rearrange("p t m j -> p m j t")
            src = w_raw[b, a][:].rearrange("p j (m t) -> p m j t", t=PACK)[:, :, :, t0:t1]
            copy(dst, src, on_vector)

        def quantize_w1(b, a, t0=0, t1=PACK):
            values = w_bf[b, a][:, t0:t1, :, :].rearrange("p t m j -> p (t m j)")
            cols = slice(t0 * P, t1 * P)
            nc.vector.quantize_mx(out=w_codes[:, b, a, cols].bitcast(FP8X4), scales=w_sc[:, b, a, cols], in_=values)

        def gather_words(a, lo, hi):
            nc.vector.tensor_copy(v_w[a][:, lo:hi], tab_w[a][:].bitcast(U32).indirect(picks(lo, hi)))

        sig_plane = {}
        sig_half = {}

        def hidden(i, half):
            b, t = divmod(i, PACK)
            cols = slice(half * HALF, (half + 1) * HALF)
            acc = psum.tile([P, HALF], F32, name=f"acc{i}_{half}", offset=((2 * i + half) % 4 + 4 * b) * BANK)
            for a in range(PASSES):
                nc.tensor.matmul_mx(
                    out=acc[:],
                    lhsT=w_codes[:, b, a, t * P : (t + 1) * P].bitcast(FP8X4),
                    lhsT_scale=w_sc[:, b, a, t * P : (t + 1) * P],
                    rhs=v_w[a][:, cols].bitcast(FP8X4),
                    rhs_scale=v_sc[4 * a : P, cols],
                    start=(a == 0),
                    stop=(a == PASSES - 1),
                )
            at = RAW_AT + 2 * SLOT if i == PACK - 1 else SIG_AT + i * SIG_BYTES
            if i >= SPLIT_FROM:
                tile = placed.tile([P, HALF], F32, name=f"sig{i}_{half}", align_bytes=64, offset=at + half * SIG_BYTES // 2)
                sig_half[i, half] = tile[:]
            else:
                if half == 0:
                    sig_plane[i] = placed.tile([P, S], F32, name=f"sig{i}", align_bytes=64, offset=at)
                sig_half[i, half] = sig_plane[i][:, cols]
            nc.scalar.activation(out=sig_half[i, half], in_=acc[:], func=ACT.Sigmoid, bias=b1_sb[:, b, t : t + 1])

        shared = keep.tile([P, PACK * S + 3 * QUARTER], F32, name="shared", align_bytes=64)
        h32 = [
            keep.tile([P, PACK, S], F32, name="h32_0", align_bytes=64),
            shared[:, 0 : PACK * S].rearrange("p (t s) -> p t s", t=PACK),
        ]
        h_bf = [
            placed.tile([P, S, PACK], BF16, name="h_bf0", align_bytes=64, offset=RAW_AT),
        ]
        late = {
            0: shared[:, PACK * S - QUARTER : PACK * S + 3 * QUARTER].bitcast(BF16).rearrange("p (j t) -> p j t", t=PACK),
            HALF: keep.tile([P, HALF, PACK], BF16, name="late_second", align_bytes=64),
        }

        def rounded(b, lo, hi):
            if b == 0:
                return h_bf[0][:, lo:hi, :]
            base = lo // HALF * HALF
            return late[base][:, lo - base : hi - base, :]

        h_codes = {}
        h_sc = keep.tile([P, PASSES, S], U8, name="h_sc", align_bytes=64)

        def gate(i, lo, hi):
            b, t = divmod(i, PACK)
            if i >= SPLIT_FROM:
                values = sig_half[i, lo // HALF][:, lo % HALF : lo % HALF + hi - lo]
            else:
                values = sig_plane[i][:, lo:hi]
            nc.vector.tensor_tensor(h32[b][:, t, lo:hi], gates[i][:].indirect(picks(lo, hi)), values, ALU.mult)

        def round_h(b, lo, hi, on_vector, t0=0, t1=PACK):
            if t1 - t0 == PACK:
                dst = rounded(b, lo, hi).rearrange("p (c i) t -> p c t i", i=4)
                src = h32[b][:, :, lo:hi].rearrange("p t (c i) -> p c t i", i=4)
            else:
                dst = rounded(b, lo, hi)[:, :, t0:t1]
                src = h32[b][:, t0:t1, lo:hi].rearrange("p t j -> p j t")
            copy(dst, src, on_vector)

        def quantize_h(b, lo, hi):
            half = lo // HALF
            if (b, half) not in h_codes:
                name = f"h_codes{b}{half}"
                if b == 0:
                    h_codes[b, half] = placed.tile([P, HALF], U32, name=name, align_bytes=64, offset=SIG_AT + SPLIT_FROM * SIG_BYTES + half * (SIG_BYTES + SIG_BYTES // 2))
                else:
                    h_codes[b, half] = keep.tile([P, HALF], U32, name=name, align_bytes=64)
            codes = h_codes[b, half][:, lo - half * HALF : hi - half * HALF]
            values = rounded(b, lo, hi).rearrange("p s t -> p (s t)")
            nc.vector.quantize_mx(out=codes.bitcast(FP8X4), scales=h_sc[:, b, lo:hi], in_=values)

        sums = {}

        def project(b, half):
            cols = slice(half * HALF, (half + 1) * HALF)
            for c in range(N // P):
                if b == 0:
                    sums[c, half] = psum.tile([P, HALF], F32, name=f"total{c}_{half}", offset=(4 * half + c) * BANK)
                nc.tensor.matmul_mx(
                    out=sums[c, half][:],
                    lhsT=w4_w[:, b, :].bitcast(U8)[:, 2 * c * P : 2 * (c + 1) * P].bitcast(FP4X4),
                    lhsT_scale=w4_sc[:, b, :].bitcast(U8)[:, c * P : (c + 1) * P],
                    rhs=h_codes[b, half][:].bitcast(FP8X4),
                    rhs_scale=h_sc[:, b, cols],
                    start=(b == 0),
                    stop=(b == PASSES - 1),
                )

        banks = {}

        def project_quarter(b, q):
            for pair in range(2):
                if b == 0:
                    banks[q, pair] = psum.tile([P, 2, QUARTER], F32, name=f"bank{q}_{pair}", offset=(2 * q + pair) * BANK)
                for k in range(2):
                    c = 2 * pair + k
                    for n in range(2):
                        cols = slice(q * QUARTER + n * P, q * QUARTER + (n + 1) * P)
                        nc.tensor.matmul_mx(
                            out=banks[q, pair][:, k, n * P : (n + 1) * P],
                            lhsT=w4_w[:, b, :].bitcast(U8)[:, 2 * c * P : 2 * (c + 1) * P].bitcast(FP4X4),
                            lhsT_scale=w4_sc[:, b, :].bitcast(U8)[:, c * P : (c + 1) * P],
                            rhs=h_codes[b, 0][:, cols].bitcast(FP8X4),
                            rhs_scale=h_sc[:, b, cols],
                            start=(b == 0 and k == 0 and n == 0),
                            stop=(b == PASSES - 1 and k == 1 and n == 1),
                        )

        def finish_quarter(q, pair):
            dst = placed.tile([P, 2, QUARTER], F32, name=f"result_q{q}_{pair}", align_bytes=64, offset=RESULT_AT[0] + BANK * (2 * q + pair))
            for k in range(2):
                nc.scalar.activation(out=dst[:, k, :], in_=banks[q, pair][:, k, :], func=ACT.Identity, bias=b2_sb[:, 2 * pair + k, 0:1])
            rows = out[2 * pair * P : 2 * (pair + 1) * P, q * QUARTER : (q + 1) * QUARTER].rearrange("(k p) j -> p k j", p=P)
            if (q, pair) == (0, 0):
                for k in range(2):
                    nc.sync.dma_start(out=rows[:, k, :], in_=dst[:, k, :])
            else:
                nc.sync.dma_start(out=rows, in_=dst[:])

        results = {}

        def finish(c, half, on_vector):
            if half not in results:
                results[half] = placed.tile([P, N // P, HALF], F32, name=f"result{half}", align_bytes=64, offset=RESULT_AT[half])
            width = HALF if c < 2 else QUARTER
            for lo in range(0, HALF, width):
                dst = results[half][:, c, lo : lo + width]
                src = sums[c, half][:, lo : lo + width]
                if on_vector:
                    nc.vector.tensor_scalar(out=dst, in0=src, scalar1=b2_sb[:, c, 0:1], scalar2=None, op0=ALU.add)
                else:
                    nc.scalar.activation(out=dst, in_=src, func=ACT.Identity, bias=b2_sb[:, c, 0:1])
                nc.sync.dma_start(out=out[c * P : (c + 1) * P, half * HALF + lo : half * HALF + lo + width], in_=dst)

        gather_words(0, 0, S)
        nc.vector.tensor_copy(v_sc[:], tab_sc[:].bitcast(U8).indirect(offsets[:]))
        round_w1(0, 0, 0, 4, False)
        quantize_w1(0, 0)
        round_w1(0, 1, 0, 2, False)
        round_w1(0, 1, 2, 4, True)
        quantize_w1(0, 1)
        gather_words(1, 0, HALF)
        gather_words(1, HALF, S)
        round_w1(1, 0, 0, 2, True)
        round_w1(1, 0, 2, 4, True)
        quantize_w1(1, 0, 0, 2)
        quantize_w1(1, 0, 2, 4)

        for i in range(PACK - 1):
            hidden(i, 0)
            hidden(i, 1)
        gate(0, 0, S)
        round_w1(1, 1, 0, 2, False)
        round_w1(1, 1, 2, 4, True)
        quantize_w1(1, 1, 2, 4)
        quantize_w1(1, 1, 0, 2)
        hidden(PACK - 1, 0)
        hidden(PACK - 1, 1)
        gate(1, 0, S)
        gate(2, 0, S)
        for i in range(PACK, PLANES):
            hidden(i, 0)
            hidden(i, 1)
        gate(3, 0, HALF)
        gate(3, HALF, S)
        round_h(0, 0, HALF, False)
        gate(4, 0, S)
        gate(5, 0, HALF)
        gate(5, HALF, S)
        round_h(0, HALF, S, False)
        round_h(1, 0, HALF, False, 0, 2)
        round_h(1, HALF, S, False, 0, 2)
        gate(6, 0, HALF)
        gate(6, HALF, S)
        quantize_h(0, 0, HALF)
        project_quarter(0, 0)
        project_quarter(0, 1)

        last = PLANES - 1
        for lo, hi in ((0, CHUNK), (CHUNK, QUARTER), (QUARTER, HALF)):
            gate(last, lo, hi)
            round_h(1, lo, hi, False, 2, 4)
            if hi % QUARTER == 0:
                quantize_h(1, hi - QUARTER, hi)
                project_quarter(1, lo // QUARTER)
        gate(last, HALF, HALF + QUARTER)
        round_h(1, HALF, HALF + QUARTER, False, 2, 4)
        gate(last, HALF + QUARTER, S)
        quantize_h(0, HALF, S)
        project(0, 1)
        round_h(1, HALF + QUARTER, S, True, 2, 4)
        quantize_h(1, HALF, HALF + QUARTER)
        quantize_h(1, HALF + QUARTER, S)
        project(1, 1)

        for q in range(2):
            for pair in range(2):
                finish_quarter(q, pair)
        for c in range(N // P):
            finish(c, 1, c % 2 == 0)
